import numpy as np
import ml_dtypes

BF16 = ml_dtypes.bfloat16


def bf(x):
    return np.asarray(x, np.float32).astype(BF16)


def f32(x):
    return np.asarray(x, np.float32)


def f64(x):
    return np.asarray(x).astype(np.float64)


def striped(idx):
    return np.tile(idx.reshape(-1, 16).T, (8, 1))


def rows(idx, k):
    return np.tile(idx, (k, 1))


def look(tab, idx):
    return np.take_along_axis(f64(tab), rows(idx, len(tab)), axis=1)


K, S, V, N = 256, 2048, 512, 512


def setup_inputs():
    return {"tab": f32(np.random.standard_normal((2, K, S))), "y": f32(1.0 * np.random.standard_normal((K, V))), "offs": striped(np.random.permutation(S)[:N])}


def reference(tab, y, offs):
    idx = offs[:16].T.reshape(-1)
    x = look(tab[0], idx) / (1.0 + np.exp(-look(tab[0], idx))) * f64(y) + look(tab[1], idx)
    return x

@@ -1,0 +1,48 @@
+import concourse.mybir as mybir
+
+F32 = mybir.dt.float32
+U16 = mybir.dt.uint16
+MULT = mybir.AluOpType.mult
+ADD = mybir.AluOpType.add
+SILU = mybir.ActivationFunctionType.Silu
+
+P = 128
+PIECES = 4
+
+
+def tile_lookup_resglu_out_kernel(tc, tab, y, offs, out):
+    nc = tc.nc
+    planes, rows, places = tab.shape
+    n = y.shape[1]
+    blocks = rows // P
+
+    with (
+        tc.tile_pool(name="lists", bufs=1) as lists,
+        tc.tile_pool(name="data", bufs=blocks) as data,
+    ):
+        gates = [data.tile([P, places], F32, name=f"gate{b}") for b in range(blocks)]
+        shifts = [data.tile([P, places], F32, name=f"shift{b}") for b in range(blocks)]
+        stream = data.tile([P, blocks, n], F32, name="stream")
+        offsets = lists.tile([P, n // 16], U16, name="offsets")
+
+        nc.sync.dma_start(gates[0][:], tab[0, :P, :])
+        nc.sync.dma_start(offsets[:], offs)
+        nc.sync.dma_start(stream[:], y.rearrange("(b p) n -> p b n", p=P))
+        for b in range(1, blocks):
+            nc.sync.dma_start(gates[b][:], tab[0, b * P : (b + 1) * P, :])
+        for b in range(blocks):
+            nc.sync.dma_start(shifts[b][:], tab[1, b * P : (b + 1) * P, :])
+
+        for b in range(blocks):
+            block = slice(b * P, (b + 1) * P)
+            opened = data.tile([P, n], F32, name="opened")
+            nc.scalar.activation(opened[:], gates[b][:].indirect(offsets[:]), SILU)
+            gated = data.tile([P, n], F32, name="gated")
+            nc.vector.tensor_tensor(gated[:], opened[:], stream[:, b, :], MULT)
+            for piece in range(PIECES):
+                width = n // PIECES
+                cols = slice(piece * width, (piece + 1) * width)
+                entries = slice(cols.start // 16, cols.stop // 16)
+                x = data.tile([P, width], F32, name=f"x{piece}")
+                nc.vector.tensor_tensor(x[:], shifts[b][:].indirect(offsets[:, entries]), gated[:, cols], ADD)
+                nc.sync.dma_start(out[block, cols], x[:])

@@ -15,6 +15,8 @@ def tile_lookup_resglu_out_kernel(tc, tab, y, offs, out):
     planes, rows, places = tab.shape
     n = y.shape[1]
     blocks = rows // P
+    tab = tab.rearrange("t (p b) s -> t b p s", b=blocks)
+    out = out.rearrange("(p b) n -> b p n", b=blocks)
 
     with (
         tc.tile_pool(name="lists", bufs=1) as lists,
@@ -25,16 +27,15 @@ def tile_lookup_resglu_out_kernel(tc, tab, y, offs, out):
         stream = data.tile([P, blocks, n], F32, name="stream")
         offsets = lists.tile([P, n // 16], U16, name="offsets")
 
-        nc.sync.dma_start(gates[0][:], tab[0, :P, :])
+        nc.sync.dma_start(gates[0][:], tab[0, 0])
         nc.sync.dma_start(offsets[:], offs)
-        nc.sync.dma_start(stream[:], y.rearrange("(b p) n -> p b n", p=P))
+        nc.sync.dma_start(stream[:], y.rearrange("(p b) n -> p b n", b=blocks))
         for b in range(1, blocks):
-            nc.sync.dma_start(gates[b][:], tab[0, b * P : (b + 1) * P, :])
+            nc.sync.dma_start(gates[b][:], tab[0, b])
         for b in range(blocks):
-            nc.sync.dma_start(shifts[b][:], tab[1, b * P : (b + 1) * P, :])
+            nc.sync.dma_start(shifts[b][:], tab[1, b])
 
         for b in range(blocks):
-            block = slice(b * P, (b + 1) * P)
             opened = data.tile([P, n], F32, name="opened")
             nc.scalar.activation(opened[:], gates[b][:].indirect(offsets[:]), SILU)
             gated = data.tile([P, n], F32, name="gated")
@@ -45,4 +46,4 @@ def tile_lookup_resglu_out_kernel(tc, tab, y, offs, out):
                 entries = slice(cols.start // 16, cols.stop // 16)
                 x = data.tile([P, width], F32, name=f"x{piece}")
                 nc.vector.tensor_tensor(x[:], shifts[b][:].indirect(offsets[:, entries]), gated[:, cols], ADD)
-                nc.sync.dma_start(out[block, cols], x[:])
+                nc.sync.dma_start(out[b, :, cols], x[:])

@@ -7,7 +7,7 @@ ADD = mybir.AluOpType.add
 SILU = mybir.ActivationFunctionType.Silu
 
 P = 128
-PIECES = 4
+CUTS = ((0, 512), (0, 128, 256, 384, 512))
 
 
 def tile_lookup_resglu_out_kernel(tc, tab, y, offs, out):
@@ -29,9 +29,9 @@ def tile_lookup_resglu_out_kernel(tc, tab, y, offs, out):
 
         nc.sync.dma_start(gates[0][:], tab[0, 0])
         nc.sync.dma_start(offsets[:], offs)
-        nc.sync.dma_start(stream[:], y.rearrange("(p b) n -> p b n", b=blocks))
         for b in range(1, blocks):
             nc.sync.dma_start(gates[b][:], tab[0, b])
+        nc.sync.dma_start(stream[:], y.rearrange("(p b) n -> p b n", b=blocks))
         for b in range(blocks):
             nc.sync.dma_start(shifts[b][:], tab[1, b])
 
@@ -40,10 +40,10 @@ def tile_lookup_resglu_out_kernel(tc, tab, y, offs, out):
             nc.scalar.activation(opened[:], gates[b][:].indirect(offsets[:]), SILU)
             gated = data.tile([P, n], F32, name="gated")
             nc.vector.tensor_tensor(gated[:], opened[:], stream[:, b, :], MULT)
-            for piece in range(PIECES):
-                width = n // PIECES
-                cols = slice(piece * width, (piece + 1) * width)
-                entries = slice(cols.start // 16, cols.stop // 16)
-                x = data.tile([P, width], F32, name=f"x{piece}")
+            for start, stop in zip(CUTS[b], CUTS[b][1:]):
+                cols = slice(start, stop)
+                entries = slice(start // 16, stop // 16)
+                x = data.tile([P, stop - start], F32, name=f"x{b}_{start}")
                 nc.vector.tensor_tensor(x[:], shifts[b][:].indirect(offsets[:, entries]), gated[:, cols], ADD)
-                nc.sync.dma_start(out[b, :, cols], x[:])
+                queue = nc.scalar if start > 0 else nc.sync
+                queue.dma_start(out[b, :, cols], x[:])

@@ -7,7 +7,7 @@ ADD = mybir.AluOpType.add
 SILU = mybir.ActivationFunctionType.Silu
 
 P = 128
-CUTS = ((0, 512), (0, 128, 256, 384, 512))
+CUTS = ((0, 128, 256, 384, 512), (0, 128, 256, 384, 512))
 
 
 def tile_lookup_resglu_out_kernel(tc, tab, y, offs, out):
@@ -35,15 +35,16 @@ def tile_lookup_resglu_out_kernel(tc, tab, y, offs, out):
         for b in range(blocks):
             nc.sync.dma_start(shifts[b][:], tab[1, b])
 
+        opened = data.tile([P, blocks, n], F32, name="opened")
         for b in range(blocks):
-            opened = data.tile([P, n], F32, name="opened")
-            nc.scalar.activation(opened[:], gates[b][:].indirect(offsets[:]), SILU)
-            gated = data.tile([P, n], F32, name="gated")
-            nc.vector.tensor_tensor(gated[:], opened[:], stream[:, b, :], MULT)
+            nc.scalar.activation(opened[:, b, :], gates[b][:].indirect(offsets[:]), SILU)
+        gated = data.tile([P, blocks, n], F32, name="gated")
+        nc.vector.tensor_tensor(gated[:], opened[:], stream[:], MULT)
+
+        for b in range(blocks):
             for start, stop in zip(CUTS[b], CUTS[b][1:]):
                 cols = slice(start, stop)
                 entries = slice(start // 16, stop // 16)
                 x = data.tile([P, stop - start], F32, name=f"x{b}_{start}")
-                nc.vector.tensor_tensor(x[:], shifts[b][:].indirect(offsets[:, entries]), gated[:, cols], ADD)
-                queue = nc.scalar if start > 0 else nc.sync
-                queue.dma_start(out[b, :, cols], x[:])
+                nc.vector.tensor_tensor(x[:], shifts[b][:].indirect(offsets[:, entries]), gated[:, b, cols], ADD)
+                nc.sync.dma_start(out[b, :, cols], x[:])

@@ -7,7 +7,8 @@ ADD = mybir.AluOpType.add
 SILU = mybir.ActivationFunctionType.Silu
 
 P = 128
-CUTS = ((0, 128, 256, 384, 512), (0, 128, 256, 384, 512))
+LAST_CUTS = (0, 128, 256, 384, 512)
+FIRST_CUTS = (0, 64, 128, 192, 256, 384, 512)
 
 
 def tile_lookup_resglu_out_kernel(tc, tab, y, offs, out):
@@ -17,34 +18,32 @@ def tile_lookup_resglu_out_kernel(tc, tab, y, offs, out):
     blocks = rows // P
     tab = tab.rearrange("t (p b) s -> t b p s", b=blocks)
     out = out.rearrange("(p b) n -> b p n", b=blocks)
+    sum_order = list(reversed(range(blocks)))
 
-    with (
-        tc.tile_pool(name="lists", bufs=1) as lists,
-        tc.tile_pool(name="data", bufs=blocks) as data,
-    ):
+    with tc.tile_pool(name="data", bufs=1) as data:
         gates = [data.tile([P, places], F32, name=f"gate{b}") for b in range(blocks)]
         shifts = [data.tile([P, places], F32, name=f"shift{b}") for b in range(blocks)]
         stream = data.tile([P, blocks, n], F32, name="stream")
-        offsets = lists.tile([P, n // 16], U16, name="offsets")
+        offsets = data.tile([P, n // 16], U16, name="offsets")
 
         nc.sync.dma_start(gates[0][:], tab[0, 0])
         nc.sync.dma_start(offsets[:], offs)
         for b in range(1, blocks):
             nc.sync.dma_start(gates[b][:], tab[0, b])
         nc.sync.dma_start(stream[:], y.rearrange("(p b) n -> p b n", b=blocks))
-        for b in range(blocks):
+        for b in sum_order:
             nc.sync.dma_start(shifts[b][:], tab[1, b])
 
-        opened = data.tile([P, blocks, n], F32, name="opened")
+        gated = []
         for b in range(blocks):
-            nc.scalar.activation(opened[:, b, :], gates[b][:].indirect(offsets[:]), SILU)
-        gated = data.tile([P, blocks, n], F32, name="gated")
-        nc.vector.tensor_tensor(gated[:], opened[:], stream[:], MULT)
+            opened = data.tile([P, n], F32, name=f"opened{b}")
+            nc.scalar.activation(opened[:], gates[b][:].indirect(offsets[:]), SILU)
+            gated.append(data.tile([P, n], F32, name=f"gated{b}"))
+            nc.vector.tensor_tensor(gated[b][:], opened[:], stream[:, b, :], MULT)
 
-        for b in range(blocks):
-            for start, stop in zip(CUTS[b], CUTS[b][1:]):
-                cols = slice(start, stop)
-                entries = slice(start // 16, stop // 16)
+        for b, cuts in zip(sum_order, (FIRST_CUTS, LAST_CUTS)):
+            for start, stop in zip(cuts, cuts[1:]):
+                entries = offsets[:, start // 16 : stop // 16]
                 x = data.tile([P, stop - start], F32, name=f"x{b}_{start}")
-                nc.vector.tensor_tensor(x[:], shifts[b][:].indirect(offsets[:, entries]), gated[:, b, cols], ADD)
-                nc.sync.dma_start(out[b, :, cols], x[:])
+                nc.vector.tensor_tensor(x[:], shifts[b][:].indirect(entries), gated[b][:, start:stop], ADD)
+                nc.sync.dma_start(out[b, :, start:stop], x[:])

@@ -7,8 +7,9 @@ ADD = mybir.AluOpType.add
 SILU = mybir.ActivationFunctionType.Silu
 
 P = 128
+FIRST_CUTS = (0, 256, 512)
 LAST_CUTS = (0, 128, 256, 384, 512)
-FIRST_CUTS = (0, 64, 128, 192, 256, 384, 512)
+FIRST_GROUPS = (0, 64, 96, 128)
 
 
 def tile_lookup_resglu_out_kernel(tc, tab, y, offs, out):
@@ -41,9 +42,10 @@ def tile_lookup_resglu_out_kernel(tc, tab, y, offs, out):
             gated.append(data.tile([P, n], F32, name=f"gated{b}"))
             nc.vector.tensor_tensor(gated[b][:], opened[:], stream[:, b, :], MULT)
 
-        for b, cuts in zip(sum_order, (FIRST_CUTS, LAST_CUTS)):
+        for b, cuts, groups in zip(sum_order, (FIRST_CUTS, LAST_CUTS), (FIRST_GROUPS, (0, P))):
             for start, stop in zip(cuts, cuts[1:]):
                 entries = offsets[:, start // 16 : stop // 16]
                 x = data.tile([P, stop - start], F32, name=f"x{b}_{start}")
                 nc.vector.tensor_tensor(x[:], shifts[b][:].indirect(entries), gated[b][:, start:stop], ADD)
-                nc.sync.dma_start(out[b, :, start:stop], x[:])
+                for low, high in zip(groups, groups[1:]):
+                    nc.sync.dma_start(out[b, low:high, start:stop], x[low:high, :])

@@ -7,9 +7,9 @@ ADD = mybir.AluOpType.add
 SILU = mybir.ActivationFunctionType.Silu
 
 P = 128
-FIRST_CUTS = (0, 256, 512)
+FIRST_CUTS = (0, 512)
 LAST_CUTS = (0, 128, 256, 384, 512)
-FIRST_GROUPS = (0, 64, 96, 128)
+FIRST_GROUPS = (0, 16, 32, 48, 64, 96, 128)
 
 
 def tile_lookup_resglu_out_kernel(tc, tab, y, offs, out):

@@ -7,6 +7,7 @@ ADD = mybir.AluOpType.add
 SILU = mybir.ActivationFunctionType.Silu
 
 P = 128
+ALIGN = 256
 FIRST_CUTS = (0, 512)
 LAST_CUTS = (0, 128, 256, 384, 512)
 FIRST_GROUPS = (0, 16, 32, 48, 64, 96, 128)
@@ -22,10 +23,10 @@ def tile_lookup_resglu_out_kernel(tc, tab, y, offs, out):
     sum_order = list(reversed(range(blocks)))
 
     with tc.tile_pool(name="data", bufs=1) as data:
-        gates = [data.tile([P, places], F32, name=f"gate{b}") for b in range(blocks)]
-        shifts = [data.tile([P, places], F32, name=f"shift{b}") for b in range(blocks)]
-        stream = data.tile([P, blocks, n], F32, name="stream")
-        offsets = data.tile([P, n // 16], U16, name="offsets")
+        gates = [data.tile([P, places], F32, name=f"gate{b}", align_bytes=ALIGN) for b in range(blocks)]
+        shifts = [data.tile([P, places], F32, name=f"shift{b}", align_bytes=ALIGN) for b in range(blocks)]
+        stream = data.tile([P, blocks, n], F32, name="stream", align_bytes=ALIGN)
+        offsets = data.tile([P, n // 16], U16, name="offsets", align_bytes=ALIGN)
 
         nc.sync.dma_start(gates[0][:], tab[0, 0])
         nc.sync.dma_start(offsets[:], offs)
@@ -37,15 +38,15 @@ def tile_lookup_resglu_out_kernel(tc, tab, y, offs, out):
 
         gated = []
         for b in range(blocks):
-            opened = data.tile([P, n], F32, name=f"opened{b}")
+            opened = data.tile([P, n], F32, name=f"opened{b}", align_bytes=ALIGN)
             nc.scalar.activation(opened[:], gates[b][:].indirect(offsets[:]), SILU)
-            gated.append(data.tile([P, n], F32, name=f"gated{b}"))
+            gated.append(data.tile([P, n], F32, name=f"gated{b}", align_bytes=ALIGN))
             nc.vector.tensor_tensor(gated[b][:], opened[:], stream[:, b, :], MULT)
 
         for b, cuts, groups in zip(sum_order, (FIRST_CUTS, LAST_CUTS), (FIRST_GROUPS, (0, P))):
             for start, stop in zip(cuts, cuts[1:]):
                 entries = offsets[:, start // 16 : stop // 16]
-                x = data.tile([P, stop - start], F32, name=f"x{b}_{start}")
+                x = data.tile([P, stop - start], F32, name=f"x{b}_{start}", align_bytes=ALIGN)
                 nc.vector.tensor_tensor(x[:], shifts[b][:].indirect(entries), gated[b][:, start:stop], ADD)
                 for low, high in zip(groups, groups[1:]):
                     nc.sync.dma_start(out[b, low:high, start:stop], x[low:high, :])

@@ -9,8 +9,8 @@ SILU = mybir.ActivationFunctionType.Silu
 P = 128
 ALIGN = 256
 FIRST_CUTS = (0, 512)
-LAST_CUTS = (0, 128, 256, 384, 512)
-FIRST_GROUPS = (0, 16, 32, 48, 64, 96, 128)
+LAST_CUTS = (0, 256, 384, 512)
+FIRST_GROUPS = (0, 16, 32, 48, 64, 80, 96, 128)
 
 
 def tile_lookup_resglu_out_kernel(tc, tab, y, offs, out):

@@ -8,9 +8,10 @@ SILU = mybir.ActivationFunctionType.Silu
 
 P = 128
 ALIGN = 256
-FIRST_CUTS = (0, 512)
-LAST_CUTS = (0, 256, 384, 512)
-FIRST_GROUPS = (0, 16, 32, 48, 64, 80, 96, 128)
+CUTS = ((0, 384, 512), (0, 256, 384, 512))
+PRODUCT_CUTS = CUTS[-1]
+WHOLE = ((0, 1),)
+GROUPS = ((((0, 4), (1, 4), (2, 4), (3, 4)), ((0, 4), (2, 4), (1, 2))), (WHOLE,) * 3)
 
 
 def tile_lookup_resglu_out_kernel(tc, tab, y, offs, out):
@@ -20,7 +21,6 @@ def tile_lookup_resglu_out_kernel(tc, tab, y, offs, out):
     blocks = rows // P
     tab = tab.rearrange("t (p b) s -> t b p s", b=blocks)
     out = out.rearrange("(p b) n -> b p n", b=blocks)
-    sum_order = list(reversed(range(blocks)))
 
     with tc.tile_pool(name="data", bufs=1) as data:
         gates = [data.tile([P, places], F32, name=f"gate{b}", align_bytes=ALIGN) for b in range(blocks)]
@@ -30,23 +30,23 @@ def tile_lookup_resglu_out_kernel(tc, tab, y, offs, out):
 
         nc.sync.dma_start(gates[0][:], tab[0, 0])
         nc.sync.dma_start(offsets[:], offs)
-        for b in range(1, blocks):
-            nc.sync.dma_start(gates[b][:], tab[0, b])
         nc.sync.dma_start(stream[:], y.rearrange("(p b) n -> p b n", b=blocks))
-        for b in sum_order:
-            nc.sync.dma_start(shifts[b][:], tab[1, b])
+        nc.sync.dma_start(shifts[0][:], tab[1, 0])
+        nc.sync.dma_start(gates[1][:], tab[0, 1])
+        nc.sync.dma_start(shifts[1][:], tab[1, 1])
 
-        gated = []
-        for b in range(blocks):
+        for b, cuts, groups in zip(range(blocks), CUTS, GROUPS):
             opened = data.tile([P, n], F32, name=f"opened{b}", align_bytes=ALIGN)
             nc.scalar.activation(opened[:], gates[b][:].indirect(offsets[:]), SILU)
-            gated.append(data.tile([P, n], F32, name=f"gated{b}", align_bytes=ALIGN))
-            nc.vector.tensor_tensor(gated[b][:], opened[:], stream[:, b, :], MULT)
-
-        for b, cuts, groups in zip(sum_order, (FIRST_CUTS, LAST_CUTS), (FIRST_GROUPS, (0, P))):
-            for start, stop in zip(cuts, cuts[1:]):
+            head = data.tile([P, PRODUCT_CUTS[-2]], F32, name=f"head{b}", align_bytes=ALIGN)
+            tail = opened[:, : n - PRODUCT_CUTS[-2]]
+            for start, stop in zip(PRODUCT_CUTS, PRODUCT_CUTS[1:]):
+                gated = tail if stop == n else head[:, start:stop]
+                nc.vector.tensor_tensor(gated, opened[:, start:stop], stream[:, b, start:stop], MULT)
+            for start, stop, piece_groups in zip(cuts, cuts[1:], groups):
                 entries = offsets[:, start // 16 : stop // 16]
+                gated = tail if stop == n else head[:, start:stop]
                 x = data.tile([P, stop - start], F32, name=f"x{b}_{start}", align_bytes=ALIGN)
-                nc.vector.tensor_tensor(x[:], shifts[b][:].indirect(entries), gated[b][:, start:stop], ADD)
-                for low, high in zip(groups, groups[1:]):
-                    nc.sync.dma_start(out[b, low:high, start:stop], x[low:high, :])
+                nc.vector.tensor_tensor(x[:], shifts[b][:].indirect(entries), gated, ADD)
+                for first, step in piece_groups:
+                    nc.sync.dma_start(out[b, first::step, start:stop], x[first::step, :])

@@ -9,9 +9,9 @@ SILU = mybir.ActivationFunctionType.Silu
 P = 128
 ALIGN = 256
 CUTS = ((0, 384, 512), (0, 256, 384, 512))
-PRODUCT_CUTS = CUTS[-1]
+PRODUCT_CUTS = CUTS[0]
 WHOLE = ((0, 1),)
-GROUPS = ((((0, 4), (1, 4), (2, 4), (3, 4)), ((0, 4), (2, 4), (1, 2))), (WHOLE,) * 3)
+GROUPS = ((((0, 4), (1, 4), (2, 4), (3, 4)), ((0, 2), (1, 2))), (WHOLE,) * 3)
 
 
 def tile_lookup_resglu_out_kernel(tc, tab, y, offs, out):
@@ -20,19 +20,21 @@ def tile_lookup_resglu_out_kernel(tc, tab, y, offs, out):
     n = y.shape[1]
     blocks = rows // P
     tab = tab.rearrange("t (p b) s -> t b p s", b=blocks)
+    y = y.rearrange("(p b) n -> b p n", b=blocks)
     out = out.rearrange("(p b) n -> b p n", b=blocks)
 
     with tc.tile_pool(name="data", bufs=1) as data:
         gates = [data.tile([P, places], F32, name=f"gate{b}", align_bytes=ALIGN) for b in range(blocks)]
         shifts = [data.tile([P, places], F32, name=f"shift{b}", align_bytes=ALIGN) for b in range(blocks)]
-        stream = data.tile([P, blocks, n], F32, name="stream", align_bytes=ALIGN)
+        stream = [data.tile([P, n], F32, name=f"stream{b}", align_bytes=ALIGN) for b in range(blocks)]
         offsets = data.tile([P, n // 16], U16, name="offsets", align_bytes=ALIGN)
 
         nc.sync.dma_start(gates[0][:], tab[0, 0])
         nc.sync.dma_start(offsets[:], offs)
-        nc.sync.dma_start(stream[:], y.rearrange("(p b) n -> p b n", b=blocks))
+        nc.sync.dma_start(stream[0][:], y[0])
         nc.sync.dma_start(shifts[0][:], tab[1, 0])
         nc.sync.dma_start(gates[1][:], tab[0, 1])
+        nc.sync.dma_start(stream[1][:], y[1])
         nc.sync.dma_start(shifts[1][:], tab[1, 1])
 
         for b, cuts, groups in zip(range(blocks), CUTS, GROUPS):
@@ -42,7 +44,7 @@ def tile_lookup_resglu_out_kernel(tc, tab, y, offs, out):
             tail = opened[:, : n - PRODUCT_CUTS[-2]]
             for start, stop in zip(PRODUCT_CUTS, PRODUCT_CUTS[1:]):
                 gated = tail if stop == n else head[:, start:stop]
-                nc.vector.tensor_tensor(gated, opened[:, start:stop], stream[:, b, start:stop], MULT)
+                nc.vector.tensor_tensor(gated, opened[:, start:stop], stream[b][:, start:stop], MULT)
             for start, stop, piece_groups in zip(cuts, cuts[1:], groups):
                 entries = offsets[:, start // 16 : stop // 16]
                 gated = tail if stop == n else head[:, start:stop]

@@ -8,10 +8,7 @@ SILU = mybir.ActivationFunctionType.Silu
 
 P = 128
 ALIGN = 256
-CUTS = ((0, 384, 512), (0, 256, 384, 512))
-PRODUCT_CUTS = CUTS[0]
-WHOLE = ((0, 1),)
-GROUPS = ((((0, 4), (1, 4), (2, 4), (3, 4)), ((0, 2), (1, 2))), (WHOLE,) * 3)
+CUTS = ((0, 256, 512), (0, 256, 384, 512))
 
 
 def tile_lookup_resglu_out_kernel(tc, tab, y, offs, out):
@@ -19,36 +16,33 @@ def tile_lookup_resglu_out_kernel(tc, tab, y, offs, out):
     planes, rows, places = tab.shape
     n = y.shape[1]
     blocks = rows // P
+    half = n // 2
     tab = tab.rearrange("t (p b) s -> t b p s", b=blocks)
-    y = y.rearrange("(p b) n -> b p n", b=blocks)
+    y = y.rearrange("(p b) n -> p b n", b=blocks)
     out = out.rearrange("(p b) n -> b p n", b=blocks)
 
     with tc.tile_pool(name="data", bufs=1) as data:
         gates = [data.tile([P, places], F32, name=f"gate{b}", align_bytes=ALIGN) for b in range(blocks)]
         shifts = [data.tile([P, places], F32, name=f"shift{b}", align_bytes=ALIGN) for b in range(blocks)]
-        stream = [data.tile([P, n], F32, name=f"stream{b}", align_bytes=ALIGN) for b in range(blocks)]
+        stream = data.tile([P, blocks, n], F32, name="stream", align_bytes=ALIGN)
         offsets = data.tile([P, n // 16], U16, name="offsets", align_bytes=ALIGN)
+        opened = [data.tile([P, n], F32, name=f"opened{b}", align_bytes=ALIGN) for b in range(blocks)]
+        gated = [data.tile([P, n], F32, name=f"gated{b}", align_bytes=ALIGN) for b in range(blocks)]
 
         nc.sync.dma_start(gates[0][:], tab[0, 0])
         nc.sync.dma_start(offsets[:], offs)
-        nc.sync.dma_start(stream[0][:], y[0])
-        nc.sync.dma_start(shifts[0][:], tab[1, 0])
         nc.sync.dma_start(gates[1][:], tab[0, 1])
-        nc.sync.dma_start(stream[1][:], y[1])
+        nc.sync.dma_start(shifts[0][:], tab[1, 0])
+        nc.sync.dma_start(stream[:], y)
         nc.sync.dma_start(shifts[1][:], tab[1, 1])
 
-        for b, cuts, groups in zip(range(blocks), CUTS, GROUPS):
-            opened = data.tile([P, n], F32, name=f"opened{b}", align_bytes=ALIGN)
-            nc.scalar.activation(opened[:], gates[b][:].indirect(offsets[:]), SILU)
-            head = data.tile([P, PRODUCT_CUTS[-2]], F32, name=f"head{b}", align_bytes=ALIGN)
-            tail = opened[:, : n - PRODUCT_CUTS[-2]]
-            for start, stop in zip(PRODUCT_CUTS, PRODUCT_CUTS[1:]):
-                gated = tail if stop == n else head[:, start:stop]
-                nc.vector.tensor_tensor(gated, opened[:, start:stop], stream[b][:, start:stop], MULT)
-            for start, stop, piece_groups in zip(cuts, cuts[1:], groups):
+        for b in range(blocks):
+            nc.scalar.activation(opened[b][:], gates[b][:].indirect(offsets[:]), SILU)
+        for b, start, stop in ((0, 0, half), (1, 0, n), (0, half, n)):
+            nc.vector.tensor_tensor(gated[b][:, start:stop], opened[b][:, start:stop], stream[:, b, start:stop], MULT)
+        for b, cuts in zip(range(blocks), CUTS):
+            for start, stop in zip(cuts, cuts[1:]):
                 entries = offsets[:, start // 16 : stop // 16]
-                gated = tail if stop == n else head[:, start:stop]
                 x = data.tile([P, stop - start], F32, name=f"x{b}_{start}", align_bytes=ALIGN)
-                nc.vector.tensor_tensor(x[:], shifts[b][:].indirect(entries), gated, ADD)
-                for first, step in piece_groups:
-                    nc.sync.dma_start(out[b, first::step, start:stop], x[first::step, :])
+                nc.vector.tensor_tensor(x[:], shifts[b][:].indirect(entries), gated[b][:, start:stop], ADD)
+                nc.sync.dma_start(out[b, :, start:stop], x[:])

@@ -8,7 +8,10 @@ SILU = mybir.ActivationFunctionType.Silu
 
 P = 128
 ALIGN = 256
-CUTS = ((0, 256, 512), (0, 256, 384, 512))
+CUTS = ((0, 384, 512), (0, 256, 384, 512))
+PRODUCT_CUTS = CUTS[0]
+WHOLE = ((0, 1),)
+GROUPS = ((((0, 4), (1, 4), (2, 4), (3, 4)), ((0, 2), (1, 2))), (WHOLE,) * 3)
 
 
 def tile_lookup_resglu_out_kernel(tc, tab, y, offs, out):
@@ -16,33 +19,36 @@ def tile_lookup_resglu_out_kernel(tc, tab, y, offs, out):
     planes, rows, places = tab.shape
     n = y.shape[1]
     blocks = rows // P
-    half = n // 2
     tab = tab.rearrange("t (p b) s -> t b p s", b=blocks)
-    y = y.rearrange("(p b) n -> p b n", b=blocks)
+    y = y.rearrange("(p b) n -> b p n", b=blocks)
     out = out.rearrange("(p b) n -> b p n", b=blocks)
 
     with tc.tile_pool(name="data", bufs=1) as data:
         gates = [data.tile([P, places], F32, name=f"gate{b}", align_bytes=ALIGN) for b in range(blocks)]
         shifts = [data.tile([P, places], F32, name=f"shift{b}", align_bytes=ALIGN) for b in range(blocks)]
-        stream = data.tile([P, blocks, n], F32, name="stream", align_bytes=ALIGN)
+        stream = [data.tile([P, n], F32, name=f"stream{b}", align_bytes=ALIGN) for b in range(blocks)]
         offsets = data.tile([P, n // 16], U16, name="offsets", align_bytes=ALIGN)
-        opened = [data.tile([P, n], F32, name=f"opened{b}", align_bytes=ALIGN) for b in range(blocks)]
-        gated = [data.tile([P, n], F32, name=f"gated{b}", align_bytes=ALIGN) for b in range(blocks)]
 
         nc.sync.dma_start(gates[0][:], tab[0, 0])
         nc.sync.dma_start(offsets[:], offs)
         nc.sync.dma_start(gates[1][:], tab[0, 1])
+        nc.sync.dma_start(stream[0][:], y[0])
         nc.sync.dma_start(shifts[0][:], tab[1, 0])
-        nc.sync.dma_start(stream[:], y)
+        nc.sync.dma_start(stream[1][:], y[1])
         nc.sync.dma_start(shifts[1][:], tab[1, 1])
 
-        for b in range(blocks):
-            nc.scalar.activation(opened[b][:], gates[b][:].indirect(offsets[:]), SILU)
-        for b, start, stop in ((0, 0, half), (1, 0, n), (0, half, n)):
-            nc.vector.tensor_tensor(gated[b][:, start:stop], opened[b][:, start:stop], stream[:, b, start:stop], MULT)
-        for b, cuts in zip(range(blocks), CUTS):
-            for start, stop in zip(cuts, cuts[1:]):
+        for b, cuts, groups in zip(range(blocks), CUTS, GROUPS):
+            opened = data.tile([P, n], F32, name=f"opened{b}", align_bytes=ALIGN)
+            nc.scalar.activation(opened[:], gates[b][:].indirect(offsets[:]), SILU)
+            head = data.tile([P, PRODUCT_CUTS[-2]], F32, name=f"head{b}", align_bytes=ALIGN)
+            tail = opened[:, : n - PRODUCT_CUTS[-2]]
+            for start, stop in zip(PRODUCT_CUTS, PRODUCT_CUTS[1:]):
+                gated = tail if stop == n else head[:, start:stop]
+                nc.vector.tensor_tensor(gated, opened[:, start:stop], stream[b][:, start:stop], MULT)
+            for start, stop, piece_groups in zip(cuts, cuts[1:], groups):
                 entries = offsets[:, start // 16 : stop // 16]
+                gated = tail if stop == n else head[:, start:stop]
                 x = data.tile([P, stop - start], F32, name=f"x{b}_{start}", align_bytes=ALIGN)
-                nc.vector.tensor_tensor(x[:], shifts[b][:].indirect(entries), gated[b][:, start:stop], ADD)
-                nc.sync.dma_start(out[b, :, start:stop], x[:])
+                nc.vector.tensor_tensor(x[:], shifts[b][:].indirect(entries), gated, ADD)
+                for first, step in piece_groups:
+                    nc.sync.dma_start(out[b, first::step, start:stop], x[first::step, :])

@@ -8,10 +8,10 @@ SILU = mybir.ActivationFunctionType.Silu
 
 P = 128
 ALIGN = 256
-CUTS = ((0, 384, 512), (0, 256, 384, 512))
+CUTS = ((0, 320, 512), (0, 320, 512))
 PRODUCT_CUTS = CUTS[0]
 WHOLE = ((0, 1),)
-GROUPS = ((((0, 4), (1, 4), (2, 4), (3, 4)), ((0, 2), (1, 2))), (WHOLE,) * 3)
+GROUPS = ((((0, 4), (1, 4), (2, 4), (3, 4)), ((0, 2), (1, 4), (3, 4))), (WHOLE,) * 2)
 
 
 def tile_lookup_resglu_out_kernel(tc, tab, y, offs, out):

@@ -8,10 +8,8 @@ SILU = mybir.ActivationFunctionType.Silu
 
 P = 128
 ALIGN = 256
-CUTS = ((0, 320, 512), (0, 320, 512))
-PRODUCT_CUTS = CUTS[0]
-WHOLE = ((0, 1),)
-GROUPS = ((((0, 4), (1, 4), (2, 4), (3, 4)), ((0, 2), (1, 4), (3, 4))), (WHOLE,) * 2)
+CUT = 320
+SHORT = 256
 
 
 def tile_lookup_resglu_out_kernel(tc, tab, y, offs, out):
@@ -20,35 +18,40 @@ def tile_lookup_resglu_out_kernel(tc, tab, y, offs, out):
     n = y.shape[1]
     blocks = rows // P
     tab = tab.rearrange("t (p b) s -> t b p s", b=blocks)
-    y = y.rearrange("(p b) n -> b p n", b=blocks)
+    y = y.rearrange("(p b) n -> p b n", b=blocks)
     out = out.rearrange("(p b) n -> b p n", b=blocks)
+    early, late = 1, 0
 
     with tc.tile_pool(name="data", bufs=1) as data:
         gates = [data.tile([P, places], F32, name=f"gate{b}", align_bytes=ALIGN) for b in range(blocks)]
         shifts = [data.tile([P, places], F32, name=f"shift{b}", align_bytes=ALIGN) for b in range(blocks)]
-        stream = [data.tile([P, n], F32, name=f"stream{b}", align_bytes=ALIGN) for b in range(blocks)]
+        stream = data.tile([P, blocks, n], F32, name="stream", align_bytes=ALIGN)
         offsets = data.tile([P, n // 16], U16, name="offsets", align_bytes=ALIGN)
 
         nc.sync.dma_start(gates[0][:], tab[0, 0])
         nc.sync.dma_start(offsets[:], offs)
         nc.sync.dma_start(gates[1][:], tab[0, 1])
-        nc.sync.dma_start(stream[0][:], y[0])
-        nc.sync.dma_start(shifts[0][:], tab[1, 0])
-        nc.sync.dma_start(stream[1][:], y[1])
-        nc.sync.dma_start(shifts[1][:], tab[1, 1])
+        for first in range(2):
+            nc.sync.dma_start(stream[first::2], y[first::2])
+        for first in range(2):
+            nc.sync.dma_start(shifts[early][first::2, :], tab[1, early, first::2])
+        nc.sync.dma_start(shifts[late][:, : places - SHORT], tab[1, late, :, : places - SHORT])
+        nc.sync.dma_start(shifts[late][:, places - SHORT :], tab[1, late, :, places - SHORT :])
 
-        for b, cuts, groups in zip(range(blocks), CUTS, GROUPS):
+        gated = []
+        for b in range(blocks):
             opened = data.tile([P, n], F32, name=f"opened{b}", align_bytes=ALIGN)
             nc.scalar.activation(opened[:], gates[b][:].indirect(offsets[:]), SILU)
-            head = data.tile([P, PRODUCT_CUTS[-2]], F32, name=f"head{b}", align_bytes=ALIGN)
-            tail = opened[:, : n - PRODUCT_CUTS[-2]]
-            for start, stop in zip(PRODUCT_CUTS, PRODUCT_CUTS[1:]):
-                gated = tail if stop == n else head[:, start:stop]
-                nc.vector.tensor_tensor(gated, opened[:, start:stop], stream[b][:, start:stop], MULT)
-            for start, stop, piece_groups in zip(cuts, cuts[1:], groups):
+            product = data.tile([P, n], F32, name=f"gated{b}", align_bytes=ALIGN)
+            nc.vector.tensor_tensor(product[:], opened[:], stream[:, b, :], MULT)
+            gated.append(product)
+
+        early_groups = (((0, 2), (1, 4), (3, 4)), ((0, 2), (1, 2)))
+        late_groups = (((0, 1),), ((0, 1),))
+        for b, groups in ((early, early_groups), (late, late_groups)):
+            for start, stop, piece_groups in zip((0, CUT), (CUT, n), groups):
                 entries = offsets[:, start // 16 : stop // 16]
-                gated = tail if stop == n else head[:, start:stop]
                 x = data.tile([P, stop - start], F32, name=f"x{b}_{start}", align_bytes=ALIGN)
-                nc.vector.tensor_tensor(x[:], shifts[b][:].indirect(entries), gated, ADD)
+                nc.vector.tensor_tensor(x[:], shifts[b][:].indirect(entries), gated[b][:, start:stop], ADD)
                 for first, step in piece_groups:
                     nc.sync.dma_start(out[b, first::step, start:stop], x[first::step, :])

@@ -31,12 +31,12 @@ def tile_lookup_resglu_out_kernel(tc, tab, y, offs, out):
         nc.sync.dma_start(gates[0][:], tab[0, 0])
         nc.sync.dma_start(offsets[:], offs)
         nc.sync.dma_start(gates[1][:], tab[0, 1])
-        for first in range(2):
-            nc.sync.dma_start(stream[first::2], y[first::2])
+        nc.sync.dma_start(stream[:], y)
         for first in range(2):
             nc.sync.dma_start(shifts[early][first::2, :], tab[1, early, first::2])
-        nc.sync.dma_start(shifts[late][:, : places - SHORT], tab[1, late, :, : places - SHORT])
-        nc.sync.dma_start(shifts[late][:, places - SHORT :], tab[1, late, :, places - SHORT :])
+        nc.sync.dma_start(shifts[late][0::2, :], tab[1, late, 0::2])
+        nc.sync.dma_start(shifts[late][1::2, : places - SHORT], tab[1, late, 1::2, : places - SHORT])
+        nc.sync.dma_start(shifts[late][1::2, places - SHORT :], tab[1, late, 1::2, places - SHORT :])
 
         gated = []
         for b in range(blocks):

import concourse.mybir as mybir

F32 = mybir.dt.float32
U16 = mybir.dt.uint16
MULT = mybir.AluOpType.mult
ADD = mybir.AluOpType.add
SILU = mybir.ActivationFunctionType.Silu

P = 128
ALIGN = 256
CUT = 320
SHORT = 256


def tile_lookup_resglu_out_kernel(tc, tab, y, offs, out):
    nc = tc.nc
    planes, rows, places = tab.shape
    n = y.shape[1]
    blocks = rows // P
    tab = tab.rearrange("t (p b) s -> t b p s", b=blocks)
    y = y.rearrange("(p b) n -> p b n", b=blocks)
    out = out.rearrange("(p b) n -> b p n", b=blocks)
    early, late = 1, 0

    with tc.tile_pool(name="data", bufs=1) as data:
        gates = [data.tile([P, places], F32, name=f"gate{b}", align_bytes=ALIGN) for b in range(blocks)]
        shifts = [data.tile([P, places], F32, name=f"shift{b}", align_bytes=ALIGN) for b in range(blocks)]
        stream = data.tile([P, blocks, n], F32, name="stream", align_bytes=ALIGN)
        offsets = data.tile([P, n // 16], U16, name="offsets", align_bytes=ALIGN)

        nc.sync.dma_start(gates[0][:], tab[0, 0])
        nc.sync.dma_start(offsets[:], offs)
        nc.sync.dma_start(gates[1][:], tab[0, 1])
        nc.sync.dma_start(stream[:], y)
        for first in range(2):
            nc.sync.dma_start(shifts[early][first::2, :], tab[1, early, first::2])
        nc.sync.dma_start(shifts[late][0::2, :], tab[1, late, 0::2])
        nc.sync.dma_start(shifts[late][1::2, : places - SHORT], tab[1, late, 1::2, : places - SHORT])
        nc.sync.dma_start(shifts[late][1::2, places - SHORT :], tab[1, late, 1::2, places - SHORT :])

        gated = []
        for b in range(blocks):
            opened = data.tile([P, n], F32, name=f"opened{b}", align_bytes=ALIGN)
            nc.scalar.activation(opened[:], gates[b][:].indirect(offsets[:]), SILU)
            product = data.tile([P, n], F32, name=f"gated{b}", align_bytes=ALIGN)
            nc.vector.tensor_tensor(product[:], opened[:], stream[:, b, :], MULT)
            gated.append(product)

        early_groups = (((0, 2), (1, 4), (3, 4)), ((0, 2), (1, 2)))
        late_groups = (((0, 1),), ((0, 1),))
        for b, groups in ((early, early_groups), (late, late_groups)):
            for start, stop, piece_groups in zip((0, CUT), (CUT, n), groups):
                entries = offsets[:, start // 16 : stop // 16]
                x = data.tile([P, stop - start], F32, name=f"x{b}_{start}", align_bytes=ALIGN)
                nc.vector.tensor_tensor(x[:], shifts[b][:].indirect(entries), gated[b][:, start:stop], ADD)
                for first, step in piece_groups:
                    nc.sync.dma_start(out[b, first::step, start:stop], x[first::step, :])
